import numpy as np
import ml_dtypes


def mxq(x, axis, fmt="e4m3"):
    dtype, down = {"e4m3": (ml_dtypes.float8_e4m3fn, 7), "e5m2": (ml_dtypes.float8_e5m2, 14)}[fmt]
    v = np.moveaxis(np.asarray(x, np.float32).astype(ml_dtypes.bfloat16).astype(np.float64), axis, -1)
    blocks = v.reshape(v.shape[:-1] + (-1, 32))
    amax = np.abs(blocks).max(-1, keepdims=True)
    byte = np.maximum(np.where(amax > 0, np.frexp(amax)[1] - 1 + 127, 0) - down, 1)
    scale = np.exp2(byte - 127.0)
    codes = (blocks / scale).astype(np.float32).astype(dtype).astype(np.float64)
    return np.moveaxis((codes * scale).reshape(v.shape), -1, axis)


WIDE = False


def mx_kscale(k):
    if not WIDE:
        return np.ones(k)
    levels = np.array([10, -10, 5, -5, 0])
    if k % 512:
        return np.exp2(np.random.permutation(np.resize(levels, k // 32))).repeat(32)
    a = np.empty((k // 512, 16))
    for p in range(k // 512):
        a[p, :8] = np.random.permutation(np.resize(levels, 8))
        for g in range(8):
            far = levels[np.abs(levels - a[p, g]) >= 10]
            a[p, g + 8] = far[np.random.randint(len(far))]
    return np.exp2(a.ravel()).repeat(32)


def f64(x):
    return np.asarray(x).astype(np.float64)


def striped(idx):
    return np.tile(idx.reshape(-1, 16).T, (8, 1)).astype(np.uint16)


def unstriped(offs):
    return offs[:16].T.reshape(-1).astype(np.int64)


K, T, E, C, N = 512, 512, 8, 128, 512


def by_expert(wq, xq):
    return np.concatenate([wq[e].T @ xq[:, e * C:(e + 1) * C] for e in range(E)], axis=1)


def setup_inputs():
    n = np.random.standard_normal
    s = mx_kscale(K)[:, None]
    first = np.random.permutation(np.repeat(np.arange(E), T // E))
    second = (first + 1 + np.random.permutation(np.repeat(np.arange(E - 1), -(-T // (E - 1)))[:T])) % E
    while np.bincount(second, minlength=E).max() != T // E:
        load = np.bincount(second, minlength=E); hi, lo = int(load.argmax()), int(load.argmin())
        t = np.flatnonzero((second == hi) & (first != lo))[0]; second[t] = lo
    slot_token = np.empty(E * C, np.int64); pos = np.empty((2, T), np.int64); fill = np.zeros(E, np.int64)
    place = np.stack([np.random.permutation(C) for _ in range(E)])
    for r, deal in enumerate((first, second)):
        for t in np.random.permutation(T):
            e = deal[t]; j = e * C + place[e, fill[e]]; fill[e] += 1; slot_token[j] = t; pos[r, t] = j
    g = np.random.uniform(0.2, 0.8, T)
    return {
        "xT": (n((K, T)) * s).astype(np.float32),
        "w": (n((E, K, N)) / np.sqrt(K) / s[None]).astype(np.float32),
        "gate": np.stack([np.tile(g, (N, 1)), np.tile(1.0 - g, (N, 1))]).astype(np.float32),
        "offs": striped(slot_token),
        "pos1": striped(pos[0]),
        "pos2": striped(pos[1]),
    }


def reference(xT, w, gate, offs, pos1, pos2):
    idx = unstriped(offs)
    xq = mxq(f64(xT)[:, idx], 0, "e4m3")
    y = by_expert(mxq(f64(w), 1, "e4m3"), xq)
    return f64(gate[0]) * y[:, unstriped(pos1)] + f64(gate[1]) * y[:, unstriped(pos2)]

@@ -1,0 +1,175 @@
+from contextlib import ExitStack
+
+import concourse.mybir as mybir
+
+K, T, E, C, N = 512, 512, 8, 128, 512
+FLOPS = 2 * K * N * E * C
+
+F32 = mybir.dt.float32
+BF16 = mybir.dt.bfloat16
+U32 = mybir.dt.uint32
+U16 = mybir.dt.uint16
+U8 = mybir.dt.uint8
+FP8X4 = mybir.dt.float8_e4m3fn_x4
+MULT = mybir.AluOpType.mult
+ADD = mybir.AluOpType.add
+
+P = 128
+PACK = 4
+NB = N // P
+SLOTS = E * C
+GATHER = 256
+X_VECTOR_COLS = 320
+W_VECTOR_COLS = [0, 0, 128, 256, 256, 320, 384]
+
+
+def vector_interleave(nc, dst, src, lo, hi):
+    nc.vector.tensor_copy(
+        out=dst[:, lo:hi, :].rearrange("p (c i) j -> p c j i", i=4),
+        in_=src[:, :, lo:hi].rearrange("p j (c i) -> p c j i", i=4),
+    )
+
+
+def scalar_interleave(nc, dst, src, lo, hi):
+    nc.scalar.copy(
+        out=dst[:, lo:hi, :].rearrange("p (c i) j -> p c j i", i=4),
+        in_=src[:, :, lo:hi].rearrange("p j (c i) -> p c j i", i=4),
+    )
+
+
+def quantise(nc, codes, scales, grouped, lo, hi):
+    nc.vector.quantize_mx(
+        out=codes[:, lo:hi].bitcast(FP8X4),
+        scales=scales[:, lo:hi],
+        in_=grouped[:, lo:hi, :].rearrange("p c j -> p (c j)"),
+    )
+
+
+def tile_routed_moe_kernel(tc, xT, w, gate, offs, pos1, pos2, out):
+    nc = tc.nc
+    with ExitStack() as ctx:
+        lists = ctx.enter_context(tc.tile_pool(name="lists", bufs=1))
+        keep = ctx.enter_context(tc.tile_pool(name="keep", bufs=1))
+        psum = ctx.enter_context(tc.psum_pool(name="psum", bufs=1))
+
+        x_raw = keep.tile([P, PACK, T], F32, name="x_raw")
+        nc.sync.dma_start(x_raw[:], xT.rearrange("(p j) t -> p j t", j=PACK))
+        offs_sb = lists.tile([P, SLOTS // 16], U16, name="offs_sb")
+        nc.sync.dma_start(offs_sb[:], offs)
+        w_raw = []
+        for e in range(E):
+            raw = keep.tile([P, PACK, N], F32, name="w_raw%d" % e)
+            nc.sync.dma_start(raw[:], w[e, :, :].rearrange("(p j) n -> p j n", j=PACK))
+            w_raw.append(raw)
+        pos1_sb = lists.tile([P, T // 16], U16, name="pos1_sb")
+        nc.sync.dma_start(pos1_sb[:], pos1)
+        pos2_sb = lists.tile([P, T // 16], U16, name="pos2_sb")
+        nc.sync.dma_start(pos2_sb[:], pos2)
+        pos_sb = [pos1_sb, pos2_sb]
+        gate_sb = []
+        for q in range(NB):
+            pair = []
+            for r in range(2):
+                g = keep.tile([P, T], F32, name="gate%d_%d" % (r, q))
+                nc.sync.dma_start(g[:], gate[r, q * P:(q + 1) * P, :])
+                pair.append(g)
+            gate_sb.append(pair)
+
+        warm_in = keep.tile([P, 8], F32, name="warm_in")
+        warm_out = keep.tile([P, 8], F32, name="warm_out")
+        nc.vector.memset(warm_in[:], 0.0)
+        nc.scalar.copy(out=warm_out[:], in_=warm_in[:])
+
+        x_bf = keep.tile([P, T, PACK], BF16, name="x_bf", align_bytes=64)
+        x_codes = keep.tile([P, T], U32, name="x_codes", align_bytes=64)
+        x_scales = keep.tile([P, T], U8, name="x_scales", align_bytes=64)
+        s_codes = keep.tile([P, SLOTS], U32, name="s_codes", align_bytes=64)
+        s_scales = keep.tile([P, SLOTS], U8, name="s_scales", align_bytes=64)
+        nc.gpsimd.memset(x_scales[:], 0)
+        vector_interleave(nc, x_bf, x_raw, 0, X_VECTOR_COLS)
+        scalar_interleave(nc, x_bf, x_raw, X_VECTOR_COLS, T)
+        quantise(nc, x_codes, x_scales, x_bf, 0, T)
+
+        def gather_slots(s):
+            cols = slice(s * GATHER, (s + 1) * GATHER)
+            some = offs_sb[:, s * GATHER // 16:(s + 1) * GATHER // 16]
+            nc.vector.tensor_copy(out=s_codes[:, cols], in_=x_codes[:].indirect(some))
+            nc.vector.tensor_copy(out=s_scales[:, cols], in_=x_scales[:].indirect(some))
+
+        acc = [[psum.tile([P, 4 * C], F32, name="acc%d_%d" % (q, h)) for h in range(E // 4)] for q in range(NB)]
+        y_sb = [keep.tile([P, SLOTS], F32, name="y_sb%d" % q) for q in range(NB)]
+        w_bf = [keep.tile([P, N, PACK], BF16, name="w_bf%d" % e, align_bytes=64) for e in range(E)]
+        w_codes = [keep.tile([P, N], U32, name="w_codes%d" % e, align_bytes=64) for e in range(E)]
+        w_scales = [keep.tile([P, N], U8, name="w_scales%d" % e, align_bytes=64) for e in range(E)]
+
+        def multiply(e, q):
+            feats = slice(q * P, (q + 1) * P)
+            slots = slice(e * C, (e + 1) * C)
+            nc.tensor.matmul_mx(
+                out=acc[q][e // 4][:, (e % 4) * C:(e % 4 + 1) * C],
+                lhsT=w_codes[e][:, feats].bitcast(FP8X4),
+                lhsT_scale=w_scales[e][:, feats],
+                rhs=s_codes[:, slots].bitcast(FP8X4),
+                rhs_scale=s_scales[:, slots],
+                start=True,
+                stop=True,
+            )
+
+        def empty(q, first, last):
+            h = first // 4
+            nc.scalar.copy(
+                out=y_sb[q][:, first * C:last * C],
+                in_=acc[q][h][:, (first - 4 * h) * C:(last - 4 * h) * C],
+            )
+
+        for s in range(SLOTS // GATHER):
+            gather_slots(s)
+
+        for e in range(E - 1):
+            split = W_VECTOR_COLS[e]
+            if split > 0:
+                vector_interleave(nc, w_bf[e], w_raw[e], 0, split)
+            scalar_interleave(nc, w_bf[e], w_raw[e], split, N)
+            quantise(nc, w_codes[e], w_scales[e], w_bf[e], 0, N)
+            for q in range(NB):
+                multiply(e, q)
+            if e == 5:
+                empty(0, 0, 4)
+            if e == 6:
+                empty(1, 0, 4)
+
+        e = E - 1
+        vector_interleave(nc, w_bf[e], w_raw[e], 0, P)
+        scalar_interleave(nc, w_bf[e], w_raw[e], 2 * P, 4 * P)
+        vector_interleave(nc, w_bf[e], w_raw[e], P, 2 * P)
+        quantise(nc, w_codes[e], w_scales[e], w_bf[e], 0, P)
+        multiply(e, 0)
+        quantise(nc, w_codes[e], w_scales[e], w_bf[e], P, 2 * P)
+        multiply(e, 1)
+        quantise(nc, w_codes[e], w_scales[e], w_bf[e], 2 * P, 4 * P)
+        multiply(e, 2)
+        multiply(e, 3)
+        empty(0, 4, 8)
+        empty(1, 4, 8)
+        empty(2, 0, 4)
+        empty(2, 4, 8)
+        empty(3, 0, 4)
+        empty(3, 4, 8)
+
+        prod = [[keep.tile([P, T], F32, name="prod%d_%d" % (r, q)) for r in range(2)] for q in range(NB)]
+
+        def fetch(q, r):
+            nc.vector.tensor_tensor(out=prod[q][r][:], in0=y_sb[q][:].indirect(pos_sb[r][:]), in1=gate_sb[q][r][:], op=MULT)
+
+        def finish(q):
+            res = keep.tile([P, T], F32, name="res%d" % q)
+            nc.vector.tensor_tensor(out=res[:], in0=prod[q][0][:], in1=prod[q][1][:], op=ADD)
+            nc.sync.dma_start(out[q * P:(q + 1) * P, :], res[:])
+
+        fetch(0, 0)
+        fetch(0, 1)
+        for q in range(1, NB):
+            fetch(q, 0)
+            finish(q - 1)
+            fetch(q, 1)
+        finish(NB - 1)

@@ -1,6 +1,7 @@
 from contextlib import ExitStack
 
 import concourse.mybir as mybir
+from concourse.masks import make_identity
 
 K, T, E, C, N = 512, 512, 8, 128, 512
 FLOPS = 2 * K * N * E * C
@@ -79,6 +80,8 @@ def tile_routed_moe_kernel(tc, xT, w, gate, offs, pos1, pos2, out):
         warm_out = keep.tile([P, 8], F32, name="warm_out")
         nc.vector.memset(warm_in[:], 0.0)
         nc.scalar.copy(out=warm_out[:], in_=warm_in[:])
+        ident = keep.tile([P, P], F32, name="ident")
+        make_identity(nc, ident[:])
 
         x_bf = keep.tile([P, T, PACK], BF16, name="x_bf", align_bytes=64)
         x_codes = keep.tile([P, T], U32, name="x_codes", align_bytes=64)
@@ -161,15 +164,34 @@ def tile_routed_moe_kernel(tc, xT, w, gate, offs, pos1, pos2, out):
         def fetch(q, r):
             nc.vector.tensor_tensor(out=prod[q][r][:], in0=y_sb[q][:].indirect(pos_sb[r][:]), in1=gate_sb[q][r][:], op=MULT)
 
-        def finish(q):
-            res = keep.tile([P, T], F32, name="res%d" % q)
-            nc.vector.tensor_tensor(out=res[:], in0=prod[q][0][:], in1=prod[q][1][:], op=ADD)
-            nc.sync.dma_start(out[q * P:(q + 1) * P, :], res[:])
+        res = [keep.tile([P, T], F32, name="res%d" % q) for q in range(NB)]
+
+        def add_on_vector(q, lo, hi):
+            nc.vector.tensor_tensor(out=res[q][:, lo:hi], in0=prod[q][0][:, lo:hi], in1=prod[q][1][:, lo:hi], op=ADD)
+
+        def add_on_tensor(q, lo, hi, bank):
+            total = psum.tile([P, hi - lo], F32, name=bank)
+            nc.tensor.matmul(total[:], lhsT=ident[:], rhs=prod[q][0][:, lo:hi], start=True, stop=False)
+            nc.tensor.matmul(total[:], lhsT=ident[:], rhs=prod[q][1][:, lo:hi], start=False, stop=True)
+            nc.scalar.copy(out=res[q][:, lo:hi], in_=total[:])
+
+        def store(q):
+            nc.sync.dma_start(out[q * P:(q + 1) * P, :], res[q][:])
 
         fetch(0, 0)
         fetch(0, 1)
-        for q in range(1, NB):
-            fetch(q, 0)
-            finish(q - 1)
-            fetch(q, 1)
-        finish(NB - 1)
+        add_on_tensor(0, 0, T, "acc0_0")
+        store(0)
+        fetch(1, 0)
+        fetch(1, 1)
+        add_on_tensor(1, 0, T // 2, "acc0_1")
+        fetch(2, 0)
+        add_on_vector(1, T // 2, T)
+        store(1)
+        fetch(2, 1)
+        fetch(3, 0)
+        add_on_vector(2, 0, T)
+        store(2)
+        fetch(3, 1)
+        add_on_vector(3, 0, T)
+        store(3)

@@ -21,7 +21,8 @@ NB = N // P
 SLOTS = E * C
 GATHER = 256
 X_VECTOR_COLS = 320
-W_VECTOR_COLS = [0, 0, 128, 256, 256, 320, 384]
+W_VECTOR_COLS = [0, 0, 0, 128, 192, 320, 384]
+W_GPSIMD_COLS = [128, 128, 128, 0, 0, 0, 0]
 
 
 def vector_interleave(nc, dst, src, lo, hi):
@@ -35,6 +36,17 @@ def scalar_interleave(nc, dst, src, lo, hi):
     nc.scalar.copy(
         out=dst[:, lo:hi, :].rearrange("p (c i) j -> p c j i", i=4),
         in_=src[:, :, lo:hi].rearrange("p j (c i) -> p c j i", i=4),
+    )
+
+
+def gpsimd_interleave(nc, dst, src, lo, hi):
+    nc.gpsimd.tensor_scalar(
+        out=dst[:, lo:hi, :].rearrange("p (c i) j -> p c j i", i=4),
+        in0=src[:, :, lo:hi].rearrange("p j (c i) -> p c j i", i=4),
+        scalar1=1.0,
+        scalar2=0.0,
+        op0=MULT,
+        op1=ADD,
     )
 
 
@@ -132,7 +144,10 @@ def tile_routed_moe_kernel(tc, xT, w, gate, offs, pos1, pos2, out):
             split = W_VECTOR_COLS[e]
             if split > 0:
                 vector_interleave(nc, w_bf[e], w_raw[e], 0, split)
-            scalar_interleave(nc, w_bf[e], w_raw[e], split, N)
+            helped = W_GPSIMD_COLS[e]
+            scalar_interleave(nc, w_bf[e], w_raw[e], split, N - helped)
+            if helped > 0:
+                gpsimd_interleave(nc, w_bf[e], w_raw[e], N - helped, N)
             quantise(nc, w_codes[e], w_scales[e], w_bf[e], 0, N)
             for q in range(NB):
                 multiply(e, q)

@@ -190,6 +190,26 @@ def tile_routed_moe_kernel(tc, xT, w, gate, offs, pos1, pos2, out):
             nc.tensor.matmul(total[:], lhsT=ident[:], rhs=prod[q][1][:, lo:hi], start=False, stop=True)
             nc.scalar.copy(out=res[q][:, lo:hi], in_=total[:])
 
+        def add_by_transposes(q, lo, hi, bank_there, bank_back):
+            pieces = (hi - lo) // P
+            there = psum.tile([P, hi - lo], F32, name=bank_there)
+            steps = [(r, b) for r in range(2) for b in range(pieces)]
+            for i, (r, b) in enumerate(steps):
+                nc.tensor.matmul(
+                    there[:, b * P:(b + 1) * P],
+                    lhsT=prod[q][r][:, lo + b * P:lo + (b + 1) * P],
+                    rhs=ident[:],
+                    is_transpose=True,
+                    start=(i == 0),
+                    stop=(i == len(steps) - 1),
+                )
+            turned = keep.tile([P, hi - lo], F32, name="turned%d" % q)
+            nc.scalar.copy(out=turned[:], in_=there[:])
+            back = psum.tile([P, hi - lo], F32, name=bank_back)
+            for b in range(pieces):
+                nc.tensor.transpose(back[:, b * P:(b + 1) * P], turned[:, b * P:(b + 1) * P], ident[:])
+            nc.scalar.copy(out=res[q][:, lo:hi], in_=back[:])
+
         def store(q):
             nc.sync.dma_start(out[q * P:(q + 1) * P, :], res[q][:])
 
@@ -200,12 +220,13 @@ def tile_routed_moe_kernel(tc, xT, w, gate, offs, pos1, pos2, out):
         fetch(1, 0)
         fetch(1, 1)
         add_on_tensor(1, 0, T // 2, "acc0_1")
-        fetch(2, 0)
-        add_on_vector(1, T // 2, T)
+        add_by_transposes(1, T // 2, T, "acc1_0", "acc1_1")
         store(1)
+        fetch(2, 0)
         fetch(2, 1)
+        add_by_transposes(2, 0, T // 2, "acc2_0", "acc2_1")
         fetch(3, 0)
-        add_on_vector(2, 0, T)
+        add_on_vector(2, T // 2, T)
         store(2)
         fetch(3, 1)
         add_on_vector(3, 0, T)

@@ -21,8 +21,8 @@ NB = N // P
 SLOTS = E * C
 GATHER = 256
 X_VECTOR_COLS = 320
-W_VECTOR_COLS = [0, 0, 0, 128, 192, 320, 384]
-W_GPSIMD_COLS = [128, 128, 128, 0, 0, 0, 0]
+W_VECTOR_COLS = [0, 0, 0, 128, 192, 320]
+W_GPSIMD_COLS = [128, 128, 128, 0, 0, 0]
 
 
 def vector_interleave(nc, dst, src, lo, hi):
@@ -70,7 +70,10 @@ def tile_routed_moe_kernel(tc, xT, w, gate, offs, pos1, pos2, out):
         offs_sb = lists.tile([P, SLOTS // 16], U16, name="offs_sb")
         nc.sync.dma_start(offs_sb[:], offs)
         w_raw = []
-        for e in range(E):
+        last = w[E - 1, :, :].rearrange("(p j) n -> p j n", j=PACK)
+        raw_0 = keep.tile([P, PACK, P], F32, name="raw_0")
+        nc.sync.dma_start(raw_0[:], last[:, :, 0:P])
+        for e in range(E - 1):
             raw = keep.tile([P, PACK, N], F32, name="w_raw%d" % e)
             nc.sync.dma_start(raw[:], w[e, :, :].rearrange("(p j) n -> p j n", j=PACK))
             w_raw.append(raw)
@@ -79,12 +82,15 @@ def tile_routed_moe_kernel(tc, xT, w, gate, offs, pos1, pos2, out):
         pos2_sb = lists.tile([P, T // 16], U16, name="pos2_sb")
         nc.sync.dma_start(pos2_sb[:], pos2)
         pos_sb = [pos1_sb, pos2_sb]
+        raw_123 = keep.tile([P, PACK, 3 * P], F32, name="raw_123")
         gate_sb = []
         for q in range(NB):
             pair = []
             for r in range(2):
-                g = keep.tile([P, T], F32, name="gate%d_%d" % (r, q))
+                g = keep.tile([P, T], F32, name="gate%d_%d" % (r, q), align_bytes=64)
                 nc.sync.dma_start(g[:], gate[r, q * P:(q + 1) * P, :])
+                if q == 0 and r == 0:
+                    nc.sync.dma_start(raw_123[:], last[:, :, P:N])
                 pair.append(g)
             gate_sb.append(pair)
 
@@ -113,9 +119,11 @@ def tile_routed_moe_kernel(tc, xT, w, gate, offs, pos1, pos2, out):
 
         acc = [[psum.tile([P, 4 * C], F32, name="acc%d_%d" % (q, h)) for h in range(E // 4)] for q in range(NB)]
         y_sb = [keep.tile([P, SLOTS], F32, name="y_sb%d" % q) for q in range(NB)]
-        w_bf = [keep.tile([P, N, PACK], BF16, name="w_bf%d" % e, align_bytes=64) for e in range(E)]
+        w_bf = [keep.tile([P, N, PACK], BF16, name="w_bf%d" % e, align_bytes=64) for e in range(E - 2)]
         w_codes = [keep.tile([P, N], U32, name="w_codes%d" % e, align_bytes=64) for e in range(E)]
         w_scales = [keep.tile([P, N], U8, name="w_scales%d" % e, align_bytes=64) for e in range(E)]
+        bf_1 = keep.tile([P, P, PACK], BF16, name="bf_1", align_bytes=64)
+        bf_23 = keep.tile([P, 2 * P, PACK], BF16, name="bf_23", align_bytes=64)
 
         def multiply(e, q):
             feats = slice(q * P, (q + 1) * P)
@@ -130,9 +138,9 @@ def tile_routed_moe_kernel(tc, xT, w, gate, offs, pos1, pos2, out):
                 stop=True,
             )
 
-        def empty(q, first, last):
+        def empty(q, first, last, move=nc.scalar.copy):
             h = first // 4
-            nc.scalar.copy(
+            move(
                 out=y_sb[q][:, first * C:last * C],
                 in_=acc[q][h][:, (first - 4 * h) * C:(last - 4 * h) * C],
             )
@@ -140,7 +148,7 @@ def tile_routed_moe_kernel(tc, xT, w, gate, offs, pos1, pos2, out):
         for s in range(SLOTS // GATHER):
             gather_slots(s)
 
-        for e in range(E - 1):
+        for e in range(E - 2):
             split = W_VECTOR_COLS[e]
             if split > 0:
                 vector_interleave(nc, w_bf[e], w_raw[e], 0, split)
@@ -151,44 +159,21 @@ def tile_routed_moe_kernel(tc, xT, w, gate, offs, pos1, pos2, out):
             quantise(nc, w_codes[e], w_scales[e], w_bf[e], 0, N)
             for q in range(NB):
                 multiply(e, q)
-            if e == 5:
-                empty(0, 0, 4)
-            if e == 6:
-                empty(1, 0, 4)
+            if e >= 4:
+                empty(e - 4, 0, 4, nc.vector.tensor_copy)
+                empty(e - 2, 0, 4)
 
-        e = E - 1
-        vector_interleave(nc, w_bf[e], w_raw[e], 0, P)
-        scalar_interleave(nc, w_bf[e], w_raw[e], 2 * P, 4 * P)
-        vector_interleave(nc, w_bf[e], w_raw[e], P, 2 * P)
-        quantise(nc, w_codes[e], w_scales[e], w_bf[e], 0, P)
-        multiply(e, 0)
-        quantise(nc, w_codes[e], w_scales[e], w_bf[e], P, 2 * P)
-        multiply(e, 1)
-        quantise(nc, w_codes[e], w_scales[e], w_bf[e], 2 * P, 4 * P)
-        multiply(e, 2)
-        multiply(e, 3)
-        empty(0, 4, 8)
-        empty(1, 4, 8)
-        empty(2, 0, 4)
-        empty(2, 4, 8)
-        empty(3, 0, 4)
-        empty(3, 4, 8)
+        prod = [[None, None] for q in range(NB)]
 
-        prod = [[keep.tile([P, T], F32, name="prod%d_%d" % (r, q)) for r in range(2)] for q in range(NB)]
-
-        def fetch(q, r):
-            nc.vector.tensor_tensor(out=prod[q][r][:], in0=y_sb[q][:].indirect(pos_sb[r][:]), in1=gate_sb[q][r][:], op=MULT)
+        def fetch(q, r, name=None):
+            product = keep.tile([P, T], F32, name=name or "prod%d_%d" % (r, q), align_bytes=64)
+            nc.vector.tensor_tensor(out=product[:], in0=y_sb[q][:].indirect(pos_sb[r][:]), in1=gate_sb[q][r][:], op=MULT)
+            prod[q][r] = product
 
         res = [keep.tile([P, T], F32, name="res%d" % q) for q in range(NB)]
 
         def add_on_vector(q, lo, hi):
             nc.vector.tensor_tensor(out=res[q][:, lo:hi], in0=prod[q][0][:, lo:hi], in1=prod[q][1][:, lo:hi], op=ADD)
-
-        def add_on_tensor(q, lo, hi, bank):
-            total = psum.tile([P, hi - lo], F32, name=bank)
-            nc.tensor.matmul(total[:], lhsT=ident[:], rhs=prod[q][0][:, lo:hi], start=True, stop=False)
-            nc.tensor.matmul(total[:], lhsT=ident[:], rhs=prod[q][1][:, lo:hi], start=False, stop=True)
-            nc.scalar.copy(out=res[q][:, lo:hi], in_=total[:])
 
         def add_by_transposes(q, lo, hi, bank_there, bank_back):
             pieces = (hi - lo) // P
@@ -210,24 +195,55 @@ def tile_routed_moe_kernel(tc, xT, w, gate, offs, pos1, pos2, out):
                 nc.tensor.transpose(back[:, b * P:(b + 1) * P], turned[:, b * P:(b + 1) * P], ident[:])
             nc.scalar.copy(out=res[q][:, lo:hi], in_=back[:])
 
-        def store(q):
-            nc.sync.dma_start(out[q * P:(q + 1) * P, :], res[q][:])
+        def store(q, lo, hi, queue):
+            queue.dma_start(out[q * P:(q + 1) * P, lo:hi], res[q][:, lo:hi])
 
+        def quantise_blocks(e, bf, first, blocks):
+            cols = slice(first * P, (first + blocks) * P)
+            nc.vector.quantize_mx(
+                out=w_codes[e][:, cols].bitcast(FP8X4),
+                scales=w_scales[e][:, cols],
+                in_=bf[:].rearrange("p c j -> p (c j)"),
+            )
+            for q in range(first, first + blocks):
+                multiply(e, q)
+
+        bf7_0 = keep.tile([P, P, PACK], BF16, name="bf7_0", align_bytes=64)
+        vector_interleave(nc, bf7_0, raw_0, 0, P)
+        quantise_blocks(7, bf7_0, 0, 1)
+        bf6_0 = keep.tile([P, P, PACK], BF16, name="bf6_0", align_bytes=64)
+        vector_interleave(nc, bf6_0, w_raw[6][:, :, 0:P], 0, P)
+        bf6_1 = keep.tile([P, P, PACK], BF16, name="bf6_1", align_bytes=64)
+        vector_interleave(nc, bf6_1, w_raw[6][:, :, P:2 * P], 0, P)
+        bf6_23 = keep.tile([P, 2 * P, PACK], BF16, name="bf6_23", align_bytes=64)
+        scalar_interleave(nc, bf6_23, w_raw[6][:, :, 2 * P:4 * P], 0, 2 * P)
+        quantise_blocks(6, bf6_0, 0, 1)
+        empty(0, 4, 8)
+        quantise_blocks(6, bf6_1, 1, 1)
+        quantise_blocks(6, bf6_23, 2, 2)
         fetch(0, 0)
-        fetch(0, 1)
-        add_on_tensor(0, 0, T, "acc0_0")
-        store(0)
+        scalar_interleave(nc, bf_1, raw_123[:, :, 0:P], 0, P)
+        quantise_blocks(7, bf_1, 1, 1)
+        empty(1, 4, 8)
+        fetch(0, 1, "bf_1")
+        scalar_interleave(nc, bf_23, raw_123[:, :, P:3 * P], 0, P)
+        scalar_interleave(nc, bf_23, raw_123[:, :, P:3 * P], P, 2 * P)
         fetch(1, 0)
-        fetch(1, 1)
-        add_on_tensor(1, 0, T // 2, "acc0_1")
-        add_by_transposes(1, T // 2, T, "acc1_0", "acc1_1")
-        store(1)
+        quantise_blocks(7, bf_23, 2, 2)
+        empty(2, 4, 8)
+        empty(3, 4, 8)
+        fetch(1, 1, "bf_23")
+        add_by_transposes(0, 0, T, "acc2_1", "acc0_0")
+        store(0, 0, T, nc.scalar)
+        add_by_transposes(1, 0, T, "acc3_1", "acc0_1")
+        store(1, 0, T, nc.scalar)
         fetch(2, 0)
         fetch(2, 1)
-        add_by_transposes(2, 0, T // 2, "acc2_0", "acc2_1")
+        add_by_transposes(2, 0, T // 2, "acc1_0", "acc1_1")
+        store(2, 0, T // 2, nc.scalar)
         fetch(3, 0)
         add_on_vector(2, T // 2, T)
-        store(2)
+        store(2, T // 2, T, nc.sync)
         fetch(3, 1)
         add_on_vector(3, 0, T)
-        store(3)
+        store(3, 0, T, nc.sync)

@@ -195,8 +195,8 @@ def tile_routed_moe_kernel(tc, xT, w, gate, offs, pos1, pos2, out):
                 nc.tensor.transpose(back[:, b * P:(b + 1) * P], turned[:, b * P:(b + 1) * P], ident[:])
             nc.scalar.copy(out=res[q][:, lo:hi], in_=back[:])
 
-        def store(q, lo, hi, queue):
-            queue.dma_start(out[q * P:(q + 1) * P, lo:hi], res[q][:, lo:hi])
+        def store(q, queue):
+            queue.dma_start(out[q * P:(q + 1) * P, :], res[q][:])
 
         def quantise_blocks(e, bf, first, blocks):
             cols = slice(first * P, (first + blocks) * P)
@@ -233,17 +233,15 @@ def tile_routed_moe_kernel(tc, xT, w, gate, offs, pos1, pos2, out):
         empty(2, 4, 8)
         empty(3, 4, 8)
         fetch(1, 1, "bf_23")
-        add_by_transposes(0, 0, T, "acc2_1", "acc0_0")
-        store(0, 0, T, nc.scalar)
-        add_by_transposes(1, 0, T, "acc3_1", "acc0_1")
-        store(1, 0, T, nc.scalar)
+        add_by_transposes(0, 0, T, "acc1_1", "acc0_0")
+        store(0, nc.scalar)
+        add_by_transposes(1, 0, T, "acc2_1", "acc0_1")
+        store(1, nc.scalar)
         fetch(2, 0)
         fetch(2, 1)
-        add_by_transposes(2, 0, T // 2, "acc1_0", "acc1_1")
-        store(2, 0, T // 2, nc.scalar)
         fetch(3, 0)
-        add_on_vector(2, T // 2, T)
-        store(2, T // 2, T, nc.sync)
+        add_on_vector(2, 0, T)
+        store(2, nc.sync)
         fetch(3, 1)
         add_on_vector(3, 0, T)
-        store(3, 0, T, nc.sync)
+        store(3, nc.sync)

@@ -21,8 +21,9 @@ NB = N // P
 SLOTS = E * C
 GATHER = 256
 X_VECTOR_COLS = 320
-W_VECTOR_COLS = [0, 0, 0, 128, 192, 320]
-W_GPSIMD_COLS = [128, 128, 128, 0, 0, 0]
+ORDER = [0, 1, 2, 3, 5, 6, 4]
+W_VECTOR_COLS = {0: 0, 1: 0, 2: 0, 3: 128, 5: 192}
+W_GPSIMD_COLS = {0: 128, 1: 128, 2: 128, 3: 0, 5: 0}
 
 
 def vector_interleave(nc, dst, src, lo, hi):
@@ -69,14 +70,14 @@ def tile_routed_moe_kernel(tc, xT, w, gate, offs, pos1, pos2, out):
         nc.sync.dma_start(x_raw[:], xT.rearrange("(p j) t -> p j t", j=PACK))
         offs_sb = lists.tile([P, SLOTS // 16], U16, name="offs_sb")
         nc.sync.dma_start(offs_sb[:], offs)
-        w_raw = []
+        w_raw = {}
         last = w[E - 1, :, :].rearrange("(p j) n -> p j n", j=PACK)
         raw_0 = keep.tile([P, PACK, P], F32, name="raw_0")
         nc.sync.dma_start(raw_0[:], last[:, :, 0:P])
-        for e in range(E - 1):
+        for e in ORDER:
             raw = keep.tile([P, PACK, N], F32, name="w_raw%d" % e)
             nc.sync.dma_start(raw[:], w[e, :, :].rearrange("(p j) n -> p j n", j=PACK))
-            w_raw.append(raw)
+            w_raw[e] = raw
         pos1_sb = lists.tile([P, T // 16], U16, name="pos1_sb")
         nc.sync.dma_start(pos1_sb[:], pos1)
         pos2_sb = lists.tile([P, T // 16], U16, name="pos2_sb")
@@ -119,7 +120,7 @@ def tile_routed_moe_kernel(tc, xT, w, gate, offs, pos1, pos2, out):
 
         acc = [[psum.tile([P, 4 * C], F32, name="acc%d_%d" % (q, h)) for h in range(E // 4)] for q in range(NB)]
         y_sb = [keep.tile([P, SLOTS], F32, name="y_sb%d" % q) for q in range(NB)]
-        w_bf = [keep.tile([P, N, PACK], BF16, name="w_bf%d" % e, align_bytes=64) for e in range(E - 2)]
+        w_bf = {e: keep.tile([P, N, PACK], BF16, name="w_bf%d" % e, align_bytes=64) for e in ORDER[:-2]}
         w_codes = [keep.tile([P, N], U32, name="w_codes%d" % e, align_bytes=64) for e in range(E)]
         w_scales = [keep.tile([P, N], U8, name="w_scales%d" % e, align_bytes=64) for e in range(E)]
         bf_1 = keep.tile([P, P, PACK], BF16, name="bf_1", align_bytes=64)
@@ -148,7 +149,7 @@ def tile_routed_moe_kernel(tc, xT, w, gate, offs, pos1, pos2, out):
         for s in range(SLOTS // GATHER):
             gather_slots(s)
 
-        for e in range(E - 2):
+        for e in ORDER[:-2]:
             split = W_VECTOR_COLS[e]
             if split > 0:
                 vector_interleave(nc, w_bf[e], w_raw[e], 0, split)
@@ -159,9 +160,9 @@ def tile_routed_moe_kernel(tc, xT, w, gate, offs, pos1, pos2, out):
             quantise(nc, w_codes[e], w_scales[e], w_bf[e], 0, N)
             for q in range(NB):
                 multiply(e, q)
-            if e >= 4:
-                empty(e - 4, 0, 4, nc.vector.tensor_copy)
-                empty(e - 2, 0, 4)
+        for q in range(2):
+            empty(q, 0, 4, nc.vector.tensor_copy)
+            empty(q + 2, 0, 4)
 
         prod = [[None, None] for q in range(NB)]
 
@@ -211,16 +212,20 @@ def tile_routed_moe_kernel(tc, xT, w, gate, offs, pos1, pos2, out):
         bf7_0 = keep.tile([P, P, PACK], BF16, name="bf7_0", align_bytes=64)
         vector_interleave(nc, bf7_0, raw_0, 0, P)
         quantise_blocks(7, bf7_0, 0, 1)
-        bf6_0 = keep.tile([P, P, PACK], BF16, name="bf6_0", align_bytes=64)
-        vector_interleave(nc, bf6_0, w_raw[6][:, :, 0:P], 0, P)
-        bf6_1 = keep.tile([P, P, PACK], BF16, name="bf6_1", align_bytes=64)
-        vector_interleave(nc, bf6_1, w_raw[6][:, :, P:2 * P], 0, P)
-        bf6_23 = keep.tile([P, 2 * P, PACK], BF16, name="bf6_23", align_bytes=64)
-        scalar_interleave(nc, bf6_23, w_raw[6][:, :, 2 * P:4 * P], 0, 2 * P)
-        quantise_blocks(6, bf6_0, 0, 1)
-        empty(0, 4, 8)
-        quantise_blocks(6, bf6_1, 1, 1)
-        quantise_blocks(6, bf6_23, 2, 2)
+        for e in ORDER[-2:]:
+            bf_b0 = keep.tile([P, P, PACK], BF16, name="bf%d_0" % e, align_bytes=64)
+            vector_interleave(nc, bf_b0, w_raw[e][:, :, 0:P], 0, P)
+            bf_b1 = keep.tile([P, P, PACK], BF16, name="bf%d_1" % e, align_bytes=64)
+            vector_interleave(nc, bf_b1, w_raw[e][:, :, P:2 * P], 0, P)
+            bf_b23 = keep.tile([P, 2 * P, PACK], BF16, name="bf%d_23" % e, align_bytes=64)
+            scalar_interleave(nc, bf_b23, w_raw[e][:, :, 2 * P:4 * P], 0, 2 * P)
+            quantise_blocks(e, bf_b0, 0, 1)
+            if e == 6:
+                empty(0, 5, 8)
+            else:
+                empty(0, 4, 5)
+            quantise_blocks(e, bf_b1, 1, 1)
+            quantise_blocks(e, bf_b23, 2, 2)
         fetch(0, 0)
         scalar_interleave(nc, bf_1, raw_123[:, :, 0:P], 0, P)
         quantise_blocks(7, bf_1, 1, 1)

from contextlib import ExitStack

import concourse.mybir as mybir
from concourse.masks import make_identity

K, T, E, C, N = 512, 512, 8, 128, 512
FLOPS = 2 * K * N * E * C

F32 = mybir.dt.float32
BF16 = mybir.dt.bfloat16
U32 = mybir.dt.uint32
U16 = mybir.dt.uint16
U8 = mybir.dt.uint8
FP8X4 = mybir.dt.float8_e4m3fn_x4
MULT = mybir.AluOpType.mult
ADD = mybir.AluOpType.add

P = 128
PACK = 4
NB = N // P
SLOTS = E * C
GATHER = 256
X_VECTOR_COLS = 320
ORDER = [0, 1, 2, 3, 5, 6, 4]
W_VECTOR_COLS = {0: 0, 1: 0, 2: 0, 3: 128, 5: 192}
W_GPSIMD_COLS = {0: 128, 1: 128, 2: 128, 3: 0, 5: 0}


def vector_interleave(nc, dst, src, lo, hi):
    nc.vector.tensor_copy(
        out=dst[:, lo:hi, :].rearrange("p (c i) j -> p c j i", i=4),
        in_=src[:, :, lo:hi].rearrange("p j (c i) -> p c j i", i=4),
    )


def scalar_interleave(nc, dst, src, lo, hi):
    nc.scalar.copy(
        out=dst[:, lo:hi, :].rearrange("p (c i) j -> p c j i", i=4),
        in_=src[:, :, lo:hi].rearrange("p j (c i) -> p c j i", i=4),
    )


def gpsimd_interleave(nc, dst, src, lo, hi):
    nc.gpsimd.tensor_scalar(
        out=dst[:, lo:hi, :].rearrange("p (c i) j -> p c j i", i=4),
        in0=src[:, :, lo:hi].rearrange("p j (c i) -> p c j i", i=4),
        scalar1=1.0,
        scalar2=0.0,
        op0=MULT,
        op1=ADD,
    )


def quantise(nc, codes, scales, grouped, lo, hi):
    nc.vector.quantize_mx(
        out=codes[:, lo:hi].bitcast(FP8X4),
        scales=scales[:, lo:hi],
        in_=grouped[:, lo:hi, :].rearrange("p c j -> p (c j)"),
    )


def tile_routed_moe_kernel(tc, xT, w, gate, offs, pos1, pos2, out):
    nc = tc.nc
    with ExitStack() as ctx:
        lists = ctx.enter_context(tc.tile_pool(name="lists", bufs=1))
        keep = ctx.enter_context(tc.tile_pool(name="keep", bufs=1))
        psum = ctx.enter_context(tc.psum_pool(name="psum", bufs=1))

        x_raw = keep.tile([P, PACK, T], F32, name="x_raw")
        nc.sync.dma_start(x_raw[:], xT.rearrange("(p j) t -> p j t", j=PACK))
        offs_sb = lists.tile([P, SLOTS // 16], U16, name="offs_sb")
        nc.sync.dma_start(offs_sb[:], offs)
        w_raw = {}
        last = w[E - 1, :, :].rearrange("(p j) n -> p j n", j=PACK)
        raw_0 = keep.tile([P, PACK, P], F32, name="raw_0")
        nc.sync.dma_start(raw_0[:], last[:, :, 0:P])
        for e in ORDER:
            raw = keep.tile([P, PACK, N], F32, name="w_raw%d" % e)
            nc.sync.dma_start(raw[:], w[e, :, :].rearrange("(p j) n -> p j n", j=PACK))
            w_raw[e] = raw
        pos1_sb = lists.tile([P, T // 16], U16, name="pos1_sb")
        nc.sync.dma_start(pos1_sb[:], pos1)
        pos2_sb = lists.tile([P, T // 16], U16, name="pos2_sb")
        nc.sync.dma_start(pos2_sb[:], pos2)
        pos_sb = [pos1_sb, pos2_sb]
        raw_123 = keep.tile([P, PACK, 3 * P], F32, name="raw_123")
        gate_sb = []
        for q in range(NB):
            pair = []
            for r in range(2):
                g = keep.tile([P, T], F32, name="gate%d_%d" % (r, q), align_bytes=64)
                nc.sync.dma_start(g[:], gate[r, q * P:(q + 1) * P, :])
                if q == 0 and r == 0:
                    nc.sync.dma_start(raw_123[:], last[:, :, P:N])
                pair.append(g)
            gate_sb.append(pair)

        warm_in = keep.tile([P, 8], F32, name="warm_in")
        warm_out = keep.tile([P, 8], F32, name="warm_out")
        nc.vector.memset(warm_in[:], 0.0)
        nc.scalar.copy(out=warm_out[:], in_=warm_in[:])
        ident = keep.tile([P, P], F32, name="ident")
        make_identity(nc, ident[:])

        x_bf = keep.tile([P, T, PACK], BF16, name="x_bf", align_bytes=64)
        x_codes = keep.tile([P, T], U32, name="x_codes", align_bytes=64)
        x_scales = keep.tile([P, T], U8, name="x_scales", align_bytes=64)
        s_codes = keep.tile([P, SLOTS], U32, name="s_codes", align_bytes=64)
        s_scales = keep.tile([P, SLOTS], U8, name="s_scales", align_bytes=64)
        nc.gpsimd.memset(x_scales[:], 0)
        vector_interleave(nc, x_bf, x_raw, 0, X_VECTOR_COLS)
        scalar_interleave(nc, x_bf, x_raw, X_VECTOR_COLS, T)
        quantise(nc, x_codes, x_scales, x_bf, 0, T)

        def gather_slots(s):
            cols = slice(s * GATHER, (s + 1) * GATHER)
            some = offs_sb[:, s * GATHER // 16:(s + 1) * GATHER // 16]
            nc.vector.tensor_copy(out=s_codes[:, cols], in_=x_codes[:].indirect(some))
            nc.vector.tensor_copy(out=s_scales[:, cols], in_=x_scales[:].indirect(some))

        acc = [[psum.tile([P, 4 * C], F32, name="acc%d_%d" % (q, h)) for h in range(E // 4)] for q in range(NB)]
        y_sb = [keep.tile([P, SLOTS], F32, name="y_sb%d" % q) for q in range(NB)]
        w_bf = {e: keep.tile([P, N, PACK], BF16, name="w_bf%d" % e, align_bytes=64) for e in ORDER[:-2]}
        w_codes = [keep.tile([P, N], U32, name="w_codes%d" % e, align_bytes=64) for e in range(E)]
        w_scales = [keep.tile([P, N], U8, name="w_scales%d" % e, align_bytes=64) for e in range(E)]
        bf_1 = keep.tile([P, P, PACK], BF16, name="bf_1", align_bytes=64)
        bf_23 = keep.tile([P, 2 * P, PACK], BF16, name="bf_23", align_bytes=64)

        def multiply(e, q):
            feats = slice(q * P, (q + 1) * P)
            slots = slice(e * C, (e + 1) * C)
            nc.tensor.matmul_mx(
                out=acc[q][e // 4][:, (e % 4) * C:(e % 4 + 1) * C],
                lhsT=w_codes[e][:, feats].bitcast(FP8X4),
                lhsT_scale=w_scales[e][:, feats],
                rhs=s_codes[:, slots].bitcast(FP8X4),
                rhs_scale=s_scales[:, slots],
                start=True,
                stop=True,
            )

        def empty(q, first, last, move=nc.scalar.copy):
            h = first // 4
            move(
                out=y_sb[q][:, first * C:last * C],
                in_=acc[q][h][:, (first - 4 * h) * C:(last - 4 * h) * C],
            )

        for s in range(SLOTS // GATHER):
            gather_slots(s)

        for e in ORDER[:-2]:
            split = W_VECTOR_COLS[e]
            if split > 0:
                vector_interleave(nc, w_bf[e], w_raw[e], 0, split)
            helped = W_GPSIMD_COLS[e]
            scalar_interleave(nc, w_bf[e], w_raw[e], split, N - helped)
            if helped > 0:
                gpsimd_interleave(nc, w_bf[e], w_raw[e], N - helped, N)
            quantise(nc, w_codes[e], w_scales[e], w_bf[e], 0, N)
            for q in range(NB):
                multiply(e, q)
        for q in range(2):
            empty(q, 0, 4, nc.vector.tensor_copy)
            empty(q + 2, 0, 4)

        prod = [[None, None] for q in range(NB)]

        def fetch(q, r, name=None):
            product = keep.tile([P, T], F32, name=name or "prod%d_%d" % (r, q), align_bytes=64)
            nc.vector.tensor_tensor(out=product[:], in0=y_sb[q][:].indirect(pos_sb[r][:]), in1=gate_sb[q][r][:], op=MULT)
            prod[q][r] = product

        res = [keep.tile([P, T], F32, name="res%d" % q) for q in range(NB)]

        def add_on_vector(q, lo, hi):
            nc.vector.tensor_tensor(out=res[q][:, lo:hi], in0=prod[q][0][:, lo:hi], in1=prod[q][1][:, lo:hi], op=ADD)

        def add_by_transposes(q, lo, hi, bank_there, bank_back):
            pieces = (hi - lo) // P
            there = psum.tile([P, hi - lo], F32, name=bank_there)
            steps = [(r, b) for r in range(2) for b in range(pieces)]
            for i, (r, b) in enumerate(steps):
                nc.tensor.matmul(
                    there[:, b * P:(b + 1) * P],
                    lhsT=prod[q][r][:, lo + b * P:lo + (b + 1) * P],
                    rhs=ident[:],
                    is_transpose=True,
                    start=(i == 0),
                    stop=(i == len(steps) - 1),
                )
            turned = keep.tile([P, hi - lo], F32, name="turned%d" % q)
            nc.scalar.copy(out=turned[:], in_=there[:])
            back = psum.tile([P, hi - lo], F32, name=bank_back)
            for b in range(pieces):
                nc.tensor.transpose(back[:, b * P:(b + 1) * P], turned[:, b * P:(b + 1) * P], ident[:])
            nc.scalar.copy(out=res[q][:, lo:hi], in_=back[:])

        def store(q, queue):
            queue.dma_start(out[q * P:(q + 1) * P, :], res[q][:])

        def quantise_blocks(e, bf, first, blocks):
            cols = slice(first * P, (first + blocks) * P)
            nc.vector.quantize_mx(
                out=w_codes[e][:, cols].bitcast(FP8X4),
                scales=w_scales[e][:, cols],
                in_=bf[:].rearrange("p c j -> p (c j)"),
            )
            for q in range(first, first + blocks):
                multiply(e, q)

        bf7_0 = keep.tile([P, P, PACK], BF16, name="bf7_0", align_bytes=64)
        vector_interleave(nc, bf7_0, raw_0, 0, P)
        quantise_blocks(7, bf7_0, 0, 1)
        for e in ORDER[-2:]:
            bf_b0 = keep.tile([P, P, PACK], BF16, name="bf%d_0" % e, align_bytes=64)
            vector_interleave(nc, bf_b0, w_raw[e][:, :, 0:P], 0, P)
            bf_b1 = keep.tile([P, P, PACK], BF16, name="bf%d_1" % e, align_bytes=64)
            vector_interleave(nc, bf_b1, w_raw[e][:, :, P:2 * P], 0, P)
            bf_b23 = keep.tile([P, 2 * P, PACK], BF16, name="bf%d_23" % e, align_bytes=64)
            scalar_interleave(nc, bf_b23, w_raw[e][:, :, 2 * P:4 * P], 0, 2 * P)
            quantise_blocks(e, bf_b0, 0, 1)
            if e == 6:
                empty(0, 5, 8)
            else:
                empty(0, 4, 5)
            quantise_blocks(e, bf_b1, 1, 1)
            quantise_blocks(e, bf_b23, 2, 2)
        fetch(0, 0)
        scalar_interleave(nc, bf_1, raw_123[:, :, 0:P], 0, P)
        quantise_blocks(7, bf_1, 1, 1)
        empty(1, 4, 8)
        fetch(0, 1, "bf_1")
        scalar_interleave(nc, bf_23, raw_123[:, :, P:3 * P], 0, P)
        scalar_interleave(nc, bf_23, raw_123[:, :, P:3 * P], P, 2 * P)
        fetch(1, 0)
        quantise_blocks(7, bf_23, 2, 2)
        empty(2, 4, 8)
        empty(3, 4, 8)
        fetch(1, 1, "bf_23")
        add_by_transposes(0, 0, T, "acc1_1", "acc0_0")
        store(0, nc.scalar)
        add_by_transposes(1, 0, T, "acc2_1", "acc0_1")
        store(1, nc.scalar)
        fetch(2, 0)
        fetch(2, 1)
        fetch(3, 0)
        add_on_vector(2, 0, T)
        store(2, nc.sync)
        fetch(3, 1)
        add_on_vector(3, 0, T)
        store(3, nc.sync)
